import numpy as np
import ml_dtypes


def mxq(x, axis, fmt="e4m3"):
    dtype, down = {"e4m3": (ml_dtypes.float8_e4m3fn, 7), "e5m2": (ml_dtypes.float8_e5m2, 14)}[fmt]
    v = np.moveaxis(np.asarray(x, np.float32).astype(ml_dtypes.bfloat16).astype(np.float64), axis, -1)
    blocks = v.reshape(v.shape[:-1] + (-1, 32))
    amax = np.abs(blocks).max(-1, keepdims=True)
    byte = np.maximum(np.where(amax > 0, np.frexp(amax)[1] - 1 + 127, 0) - down, 1)
    scale = np.exp2(byte - 127.0)
    codes = (blocks / scale).astype(np.float32).astype(dtype).astype(np.float64)
    return np.moveaxis((codes * scale).reshape(v.shape), -1, axis)


WIDE = False


def mx_kscale(k):
    if not WIDE:
        return np.ones(k)
    levels = np.array([10, -10, 5, -5, 0])
    if k % 512:
        return np.exp2(np.random.permutation(np.resize(levels, k // 32))).repeat(32)
    a = np.empty((k // 512, 16))
    for p in range(k // 512):
        a[p, :8] = np.random.permutation(np.resize(levels, 8))
        for g in range(8):
            far = levels[np.abs(levels - a[p, g]) >= 10]
            a[p, g + 8] = far[np.random.randint(len(far))]
    return np.exp2(a.ravel()).repeat(32)


def f64(x):
    return np.asarray(x).astype(np.float64)


def striped(idx):
    return np.tile(idx.reshape(-1, 16).T, (8, 1)).astype(np.uint16)


def unstriped(offs):
    return offs[:16].T.reshape(-1).astype(np.int64)


def sigmoid(v):
    return 1.0 / (1.0 + np.exp(-np.maximum(v, -700.0)))


K, T, E, C, H, N = 512, 1024, 8, 256, 512, 128


def by_expert(wq, xq):
    return np.concatenate([wq[e].T @ xq[:, e * C:(e + 1) * C] for e in range(E)], axis=1)


def setup_inputs():
    n = np.random.standard_normal
    s = mx_kscale(K)[:, None]
    u = mx_kscale(H)
    first = np.random.permutation(np.repeat(np.arange(E), T // E))
    second = (first + 1 + np.random.permutation(np.repeat(np.arange(E - 1), -(-T // (E - 1)))[:T])) % E
    while np.bincount(second, minlength=E).max() != T // E:
        load = np.bincount(second, minlength=E); hi, lo = int(load.argmax()), int(load.argmin())
        t = np.flatnonzero((second == hi) & (first != lo))[0]; second[t] = lo
    slot_token = np.empty(E * C, np.int64); pos = np.empty((2, T), np.int64); fill = np.zeros(E, np.int64)
    place = np.stack([np.random.permutation(C) for _ in range(E)])
    for r, deal in enumerate((first, second)):
        for t in np.random.permutation(T):
            e = deal[t]; j = e * C + place[e, fill[e]]; fill[e] += 1; slot_token[j] = t; pos[r, t] = j
    g = np.random.uniform(0.2, 0.8, T)
    return {
        "xT": (n((K, T)) * s).astype(np.float32),
        "w1": (n((E + 1, K, H)) / np.sqrt(K) / s[None]).astype(np.float32),
        "w3": (n((E + 1, K, H)) / np.sqrt(K) / s[None] * u[None, None, :]).astype(np.float32),
        "w2": (n((E + 1, H, N)) / np.sqrt(H) / u[None, :, None]).astype(np.float32),
        "gate": np.stack([np.tile(g, (N, 1)), np.tile(1.0 - g, (N, 1))]).astype(np.float32),
        "offs": striped(slot_token),
        "pos1": striped(pos[0]),
        "pos2": striped(pos[1]),
    }


def reference(xT, w1, w3, w2, gate, offs, pos1, pos2):
    idx = unstriped(offs)
    w1q, w3q, w2q = mxq(f64(w1), 1, "e4m3"), mxq(f64(w3), 1, "e4m3"), mxq(f64(w2), 1, "e4m3")
    xs = mxq(f64(xT), 0, "e4m3")
    hs = sigmoid(w1q[E].T @ xs) * (w3q[E].T @ xs)
    ys = w2q[E].T @ mxq(hs, 0, "e4m3")
    xq = mxq(f64(xT)[:, idx], 0, "e4m3")
    h = sigmoid(by_expert(w1q, xq))
    h = h * by_expert(w3q, xq)
    y = by_expert(w2q, mxq(h, 0, "e4m3"))
    return ys + f64(gate[0]) * y[:, unstriped(pos1)] + f64(gate[1]) * y[:, unstriped(pos2)]

@@ -1,0 +1,275 @@
+from contextlib import ExitStack
+
+import concourse.mybir as mybir
+
+K, T, E, C, H, N = 512, 1024, 8, 256, 512, 128
+FLOPS = 3623878656
+
+F32 = mybir.dt.float32
+BF16 = mybir.dt.bfloat16
+U32 = mybir.dt.uint32
+U16 = mybir.dt.uint16
+U8 = mybir.dt.uint8
+FP8X4 = mybir.dt.float8_e4m3fn_x4
+SIGMOID = mybir.ActivationFunctionType.Sigmoid
+MULT = mybir.AluOpType.mult
+ADD = mybir.AluOpType.add
+
+P = 128
+PACK = 4
+GROUP = 128
+PAIR = 2 * C
+ORDER = [0,1,2,8,3,4,5,6,7]
+W3_SCALAR = [80,80,80,80,80,80,80,80,80]
+W2_ENGINE = ["V","V","V","V","V","V","V","V","V"]
+
+
+def tile_moe_shr_glu_sigmoid_kernel(tc, xT, w1, w3, w2, gate, offs, pos1, pos2, out):
+    nc = tc.nc
+    with ExitStack() as ctx:
+        keep = ctx.enter_context(tc.tile_pool(name="keep", bufs=1))
+        rawp = ctx.enter_context(tc.tile_pool(name="rawp", bufs=6))
+        work = ctx.enter_context(tc.tile_pool(name="work", bufs=3))
+        slabs1 = ctx.enter_context(tc.tile_pool(name="slabs1", bufs=1))
+        slabs3 = ctx.enter_context(tc.tile_pool(name="slabs3", bufs=1))
+        psum = ctx.enter_context(tc.psum_pool(name="psum", bufs=2))
+
+        warm = keep.tile([P, 1], F32, name="warm")
+        warm_out = keep.tile([P, 1], F32, name="warm_out")
+        nc.gpsimd.memset(warm[:], 0.0)
+        nc.scalar.activation(out=warm_out[:], in_=warm[:], func=SIGMOID)
+
+        offs_sb = keep.tile([P, E * C // 16], U16, name="offs_sb")
+        nc.sync.dma_start(offs_sb[:], offs)
+        x_raw = keep.tile([P, PACK, T], F32, name="x_raw")
+        x_view = xT.rearrange("(p j) t -> p j t", j=PACK)
+        for u in range(2):
+            for half in range(2):
+                cols = slice(half * 512, half * 512 + 512)
+                nc.sync.dma_start(out=x_raw[:, 2 * u : 2 * u + 2, cols], in_=x_view[:, 2 * u : 2 * u + 2, cols])
+        pos1_sb = keep.tile([P, T // 16], U16, name="pos1_sb")
+        pos2_sb = keep.tile([P, T // 16], U16, name="pos2_sb")
+        gate_sb = [keep.tile([P, T], F32, name="gate0"), keep.tile([P, T], F32, name="gate1")]
+
+        raw = {}
+
+        def load(k):
+            e = ORDER[k]
+            if k == 5:
+                nc.sync.dma_start(pos1_sb[:], pos1)
+                nc.sync.dma_start(pos2_sb[:], pos2)
+                for r in range(2):
+                    nc.sync.dma_start(out=gate_sb[r][:], in_=gate[r])
+            r1 = rawp.tile([P, PACK, H], F32, name="w13_raw", tag="w13_raw")
+            nc.sync.dma_start(out=r1[:], in_=w1[e].rearrange("(p j) c -> p j c", j=PACK))
+            r3 = rawp.tile([P, PACK, H], F32, name="w13_raw", tag="w13_raw")
+            nc.sync.dma_start(out=r3[:], in_=w3[e].rearrange("(p j) c -> p j c", j=PACK))
+            r2 = rawp.tile([P, PACK, N], F32, name="w2_raw", tag="w2_raw", bufs=4)
+            nc.sync.dma_start(out=r2[:], in_=w2[e].rearrange("(p j) c -> p j c", j=PACK))
+            raw[e] = (r1, r3, r2)
+
+        windows = []
+        for u in range(2):
+            win = keep.tile([P, 2 * T], BF16, name="win%d" % u)
+            dst = win[:].rearrange("p (t e) -> p t e", e=2)
+            src = x_raw[:, 2 * u : 2 * u + 2, :].rearrange("p e t -> p t e")
+            for half in range(2):
+                cols = slice(half * 512, half * 512 + 512)
+                if 2 * u + half in [0,2]:
+                    nc.vector.tensor_copy(dst[:, cols, :], src[:, cols, :])
+                else:
+                    nc.scalar.copy(dst[:, cols, :], src[:, cols, :])
+            windows.append(win)
+
+        for k in range(3):
+            load(k)
+
+        x_shared = keep.tile([P, T, PACK], BF16, name="x_shared", align_bytes=64)
+        for part in range(4):
+            dst = x_shared[:].rearrange("p (c i) j -> p c j i", i=4)[:, part * 64 : part * 64 + 64]
+            src = x_raw[:].rearrange("p j (c i) -> p c j i", i=4)[:, part * 64 : part * 64 + 64]
+            nc.gpsimd.tensor_scalar(dst, src, 1.0, 0.0, MULT, ADD)
+
+        x_codes = {}
+
+        def quantize(src, width, name, pool, bufs):
+            codes = pool.tile([P, width], U32, name=name + "_codes", tag=name + "_codes", bufs=bufs, align_bytes=64)
+            scales = pool.tile([P, width], U8, name=name + "_scales", tag=name + "_scales", bufs=bufs, align_bytes=64)
+            nc.vector.quantize_mx(out=codes[:].bitcast(FP8X4), scales=scales[:], in_=src)
+            return codes, scales
+
+        def gather(q):
+            g = work.tile([P, PAIR, PACK], BF16, name="gathered", tag="gathered", bufs=1, align_bytes=64)
+            words = g[:].rearrange("p s j -> p (s j)").bitcast(U32).rearrange("p (s u) -> p s u", u=2)
+            for u in range(2):
+                nc.vector.tensor_copy(
+                    words[:, :, u],
+                    windows[u][:].bitcast(U32).indirect(offs_sb[:, q * PAIR // 16 : (q + 1) * PAIR // 16]),
+                )
+            x_codes[q] = quantize(g[:].rearrange("p s j -> p (s j)"), PAIR, "x", work, 2)
+
+        def copy_permuted(dst_tile, src_tile, m_scalar):
+            dst = dst_tile[:, : PACK * H].rearrange("p (t m j) -> p m j t", t=4, j=PACK)
+            src = src_tile[:].rearrange("p j (m t) -> p m j t", t=4)
+            if m_scalar > 0:
+                nc.scalar.copy(dst[:, :m_scalar], src[:, :m_scalar])
+            if m_scalar < 128:
+                nc.vector.tensor_copy(dst[:, m_scalar:], src[:, m_scalar:])
+
+        def weights1(k):
+            bf = slabs1.tile([P, PACK * H + 512], BF16, name="w1_bf%d" % k, offset=(k % 3) * 5120, align_bytes=64)
+            copy_permuted(bf, raw[ORDER[k]][0], 128)
+            return quantize(bf[:, : PACK * H], H, "w1", work, 3)
+
+        def weights3(k):
+            bf = slabs3.tile([P, PACK * H], BF16, name="w3_bf%d" % k, offset=(k % 3) * 4096, align_bytes=64)
+            copy_permuted(bf, raw[ORDER[k]][1], W3_SCALAR[k])
+            return quantize(bf[:], H, "w3", work, 3)
+
+        def weights2(e, at):
+            if at is None:
+                bf = work.tile([P, N, PACK], BF16, name="w2_bf", tag="w2_bf", bufs=2, align_bytes=64)
+            else:
+                bf = slabs1.tile([P, N, PACK], BF16, name="w2_bf%d" % e, offset=(at % 3) * 5120 + 4096, align_bytes=64)
+            dst = bf[:].rearrange("p (c i) j -> p c j i", i=4)
+            src = raw[e][2][:].rearrange("p j (c i) -> p c j i", i=4)
+            if W2_ENGINE[e] == "V":
+                nc.vector.tensor_copy(dst, src)
+            elif W2_ENGINE[e] == "S":
+                nc.scalar.copy(dst, src)
+            else:
+                nc.gpsimd.tensor_scalar(dst, src, 1.0, 0.0, MULT, ADD)
+            return quantize(bf[:].rearrange("p c j -> p (c j)"), N, "w2", work, 4)
+
+        def product(w, x, col, tag, bufs):
+            ps = psum.tile([P, PACK * GROUP], F32, name=tag, tag=tag, bufs=bufs)
+            for t in range(4):
+                nc.tensor.matmul_mx(
+                    out=ps[:, t * GROUP : (t + 1) * GROUP],
+                    lhsT=w[0][:, t * 128 : (t + 1) * 128].bitcast(FP8X4),
+                    lhsT_scale=w[1][:, t * 128 : (t + 1) * 128],
+                    rhs=x[0][:, col : col + GROUP].bitcast(FP8X4),
+                    rhs_scale=x[1][:, col : col + GROUP],
+                    start=True,
+                    stop=True,
+                )
+            return ps[:].rearrange("p (j n) -> p n j", j=PACK)
+
+        y = keep.tile([P, E * C], F32, name="y")
+        ys = keep.tile([P, T], F32, name="ys")
+        w1q, w3q, w2q, b, hq, s = {}, {}, {}, {}, {}, {}
+        shared = {}
+
+        def x_of(e):
+            return (x_codes[e // 2], (e % 2) * C)
+
+        def gate_half(e, x, col, st):
+            a = product(w1q[e], x, col, "a_ps", 2)
+            nc.scalar.activation(out=st[:], in_=a, func=SIGMOID)
+
+        def sigmoids(e, k):
+            for g in range(2):
+                if k is None:
+                    st = work.tile([P, GROUP, PACK], F32, name="s_sh", tag="s_sh", bufs=8)
+                else:
+                    st = slabs1.tile(
+                        [P, GROUP, PACK], F32, name="s%d_%d" % (e, g), offset=(k % 3) * 5120 + 2048 * g, align_bytes=64
+                    )
+                s[e, g] = st
+                x, base = x_of(e)
+                gate_half(e, x, base + g * GROUP, st)
+
+        def hidden(e, k):
+            if k is None:
+                hb = work.tile([P, C, PACK], BF16, name="hb", tag="hb", bufs=3, align_bytes=64)
+            else:
+                hb = slabs3.tile([P, C, PACK], BF16, name="hb%d" % e, offset=(k % 3) * 4096, align_bytes=64)
+            for g in range(2):
+                nc.vector.tensor_tensor(hb[:, g * GROUP : (g + 1) * GROUP, :], b[e][g], s[e, g][:], MULT)
+            hq[e] = quantize(hb[:].rearrange("p n j -> p (n j)"), 256, "h", work, 4)
+
+        def second(w, h, ps, col):
+            nc.tensor.matmul_mx(
+                out=ps[:, col : col + 256],
+                lhsT=w[0][:].bitcast(FP8X4),
+                lhsT_scale=w[1][:],
+                rhs=h[0][:].bitcast(FP8X4),
+                rhs_scale=h[1][:],
+                start=True,
+                stop=True,
+            )
+
+        def results(e):
+            y_ps = psum.tile([P, 512], F32, name="y_ps", tag="y_ps", bufs=2)
+            second(w2q[e], hq[e], y_ps, 0)
+            nc.scalar.copy(y[:, e * C : (e + 1) * C], y_ps[:, :C])
+
+        def shared_sigmoids():
+            for g in range(T // GROUP):
+                st = work.tile([P, GROUP, PACK], F32, name="s_sh", tag="s_sh", bufs=8)
+                gate_half(E, shared["x"], g * GROUP, st)
+                s[E, g] = st
+
+        def shared_hidden():
+            for i in range(T // 512):
+                y_ps = psum.tile([P, 512], F32, name="y_ps", tag="y_ps", bufs=2)
+                for h in range(2):
+                    hb = work.tile([P, C, PACK], BF16, name="hb", tag="hb", bufs=3, align_bytes=64)
+                    for g in range(2):
+                        n = i * 4 + h * 2 + g
+                        bt = product(w3q[E], shared["x"], n * GROUP, "b_ps", 4)
+                        nc.vector.tensor_tensor(hb[:, g * GROUP : (g + 1) * GROUP, :], bt, s[E, n][:], MULT)
+                    second(w2q[E], quantize(hb[:].rearrange("p n j -> p (n j)"), 256, "h", work, 4), y_ps, h * 256)
+                nc.scalar.copy(ys[:, i * 512 : (i + 1) * 512], y_ps[:])
+
+        for k in range(E + 1):
+            e = ORDER[k]
+            prev = ORDER[k - 1] if k >= 1 else None
+            if e < E and e // 2 not in x_codes:
+                gather(e // 2)
+            w1q[e] = weights1(k)
+            if prev == E:
+                w2q[E] = weights2(E, k)
+                shared_sigmoids()
+            elif k >= 1:
+                sigmoids(prev, k)
+            if k >= 2 and ORDER[k - 2] < E:
+                w2q[ORDER[k - 2]] = weights2(ORDER[k - 2], k)
+                results(ORDER[k - 2])
+            w3q[e] = weights3(k)
+            if e < E:
+                x, base = x_of(e)
+                b[e] = [product(w3q[e], x, base + g * GROUP, "b_ps", 4) for g in range(2)]
+            if prev == E:
+                shared_hidden()
+            elif k >= 1:
+                hidden(prev, k)
+            if k + 3 <= E:
+                load(k + 3)
+            if k == 1:
+                shared["x"] = quantize(x_shared[:].rearrange("p t j -> p (t j)"), T, "xs", keep, 1)
+        last = ORDER[E]
+        w2q[last] = weights2(last, None)
+        sigmoids(last, None)
+        prev = ORDER[E - 1]
+        w2q[prev] = weights2(prev, None)
+        hidden(last, None)
+        results(prev)
+        results(last)
+
+        r1 = keep.tile([P, T], F32, name="r1")
+        r2 = keep.tile([P, T], F32, name="r2")
+        r1s = keep.tile([P, T], F32, name="r1s")
+        W = T // 2
+        for i in range(2):
+            cols = slice(i * W, (i + 1) * W)
+            lst = slice(i * W // 16, (i + 1) * W // 16)
+            nc.vector.tensor_tensor(r1[:, cols], y[:].indirect(pos1_sb[:, lst]), gate_sb[0][:, cols], MULT)
+            nc.gpsimd.tensor_tensor(r1s[:, cols], r1[:, cols], ys[:, cols], ADD)
+        for i in range(2):
+            cols = slice(i * W, (i + 1) * W)
+            lst = slice(i * W // 16, (i + 1) * W // 16)
+            nc.vector.tensor_tensor(r2[:, cols], y[:].indirect(pos2_sb[:, lst]), gate_sb[1][:, cols], MULT)
+            o = work.tile([P, W], F32, name="o", tag="o", bufs=2)
+            nc.vector.tensor_tensor(o[:], r2[:, cols], r1s[:, cols], ADD)
+            nc.sync.dma_start(out=out[:, cols], in_=o[:])

@@ -19,9 +19,30 @@ P = 128
 PACK = 4
 GROUP = 128
 PAIR = 2 * C
-ORDER = [0,1,2,8,3,4,5,6,7]
-W3_SCALAR = [80,80,80,80,80,80,80,80,80]
-W2_ENGINE = ["V","V","V","V","V","V","V","V","V"]
+ORDER = [0,1,2,3,8,4,5,6,7]
+W3_SCALAR = [112,80,96,32,112,32,48,48,32]
+W2_ENGINE = ["G","V","G","G","S","S","V","S","G"]
+CAST = ["V","G","G","S"]
+W1_SCALAR = [112,112,112,128,128,128,128,128,112]
+W3_GPSIMD = [16,16,32,48,32,32,32,32,32]
+GP = 2
+SP = [2,2,2,2,2,2,1,1,1]
+CHUNKS = 2
+YS_ENGINE = "V"
+GATHER_AT = [-1,-1,3,2]
+XS_AT = 2
+FIN = ["V","V"]
+SLAG = 1
+HLAG = 1
+W2LAG = 2
+R1 = 2
+R3 = 3
+WB = 4
+XB = 4
+ABUFS = 2
+BBUFS = 4
+LOAD_AHEAD = 3
+GATE_AT = 4
 
 
 def tile_moe_shr_glu_sigmoid_kernel(tc, xT, w1, w3, w2, gate, offs, pos1, pos2, out):
@@ -55,7 +76,7 @@ def tile_moe_shr_glu_sigmoid_kernel(tc, xT, w1, w3, w2, gate, offs, pos1, pos2, 
 
         def load(k):
             e = ORDER[k]
-            if k == 5:
+            if k == GATE_AT:
                 nc.sync.dma_start(pos1_sb[:], pos1)
                 nc.sync.dma_start(pos2_sb[:], pos2)
                 for r in range(2):
@@ -75,13 +96,15 @@ def tile_moe_shr_glu_sigmoid_kernel(tc, xT, w1, w3, w2, gate, offs, pos1, pos2, 
             src = x_raw[:, 2 * u : 2 * u + 2, :].rearrange("p e t -> p t e")
             for half in range(2):
                 cols = slice(half * 512, half * 512 + 512)
-                if 2 * u + half in [0,2]:
+                if CAST[2 * u + half] == "V":
                     nc.vector.tensor_copy(dst[:, cols, :], src[:, cols, :])
+                elif CAST[2 * u + half] == "G":
+                    nc.gpsimd.tensor_scalar(dst[:, cols, :], src[:, cols, :], 1.0, 0.0, MULT, ADD)
                 else:
                     nc.scalar.copy(dst[:, cols, :], src[:, cols, :])
             windows.append(win)
 
-        for k in range(3):
+        for k in range(LOAD_AHEAD):
             load(k)
 
         x_shared = keep.tile([P, T, PACK], BF16, name="x_shared", align_bytes=64)
@@ -99,38 +122,50 @@ def tile_moe_shr_glu_sigmoid_kernel(tc, xT, w1, w3, w2, gate, offs, pos1, pos2, 
             return codes, scales
 
         def gather(q):
-            g = work.tile([P, PAIR, PACK], BF16, name="gathered", tag="gathered", bufs=1, align_bytes=64)
+            at = GATHER_AT[q]
+            if at < 0:
+                g = work.tile([P, PAIR, PACK], BF16, name="gathered", tag="gathered", bufs=1, align_bytes=64)
+            else:
+                g = slabs3.tile([P, PAIR, PACK], BF16, name="gathered%d" % q, offset=(at % R3) * 8192 + 4096, align_bytes=64)
             words = g[:].rearrange("p s j -> p (s j)").bitcast(U32).rearrange("p (s u) -> p s u", u=2)
             for u in range(2):
                 nc.vector.tensor_copy(
                     words[:, :, u],
                     windows[u][:].bitcast(U32).indirect(offs_sb[:, q * PAIR // 16 : (q + 1) * PAIR // 16]),
                 )
-            x_codes[q] = quantize(g[:].rearrange("p s j -> p (s j)"), PAIR, "x", work, 2)
+            x_codes[q] = quantize(g[:].rearrange("p s j -> p (s j)"), PAIR, "x", work, XB)
 
-        def copy_permuted(dst_tile, src_tile, m_scalar):
+        def copy_permuted(dst_tile, src_tile, m_scalar, m_gpsimd, pieces):
             dst = dst_tile[:, : PACK * H].rearrange("p (t m j) -> p m j t", t=4, j=PACK)
             src = src_tile[:].rearrange("p j (m t) -> p m j t", t=4)
+            m_vector = max(m_scalar, 128 - m_gpsimd)
             if m_scalar > 0:
-                nc.scalar.copy(dst[:, :m_scalar], src[:, :m_scalar])
-            if m_scalar < 128:
-                nc.vector.tensor_copy(dst[:, m_scalar:], src[:, m_scalar:])
+                step = m_scalar // pieces
+                for i in range(pieces):
+                    nc.scalar.copy(dst[:, i * step : (i + 1) * step], src[:, i * step : (i + 1) * step])
+            if m_scalar < m_vector:
+                nc.vector.tensor_copy(dst[:, m_scalar:m_vector], src[:, m_scalar:m_vector])
+            if m_vector < 128:
+                step = (128 - m_vector) // GP
+                for i in range(GP):
+                    a = m_vector + i * step
+                    nc.gpsimd.tensor_scalar(dst[:, a : a + step], src[:, a : a + step], 1.0, 0.0, MULT, ADD)
 
         def weights1(k):
-            bf = slabs1.tile([P, PACK * H + 512], BF16, name="w1_bf%d" % k, offset=(k % 3) * 5120, align_bytes=64)
-            copy_permuted(bf, raw[ORDER[k]][0], 128)
-            return quantize(bf[:, : PACK * H], H, "w1", work, 3)
+            bf = slabs1.tile([P, PACK * H + 512], BF16, name="w1_bf%d" % k, offset=(k % R1) * 5120, align_bytes=64)
+            copy_permuted(bf, raw[ORDER[k]][0], W1_SCALAR[k], 0, SP[k])
+            return quantize(bf[:, : PACK * H], H, "w1", work, WB)
 
         def weights3(k):
-            bf = slabs3.tile([P, PACK * H], BF16, name="w3_bf%d" % k, offset=(k % 3) * 4096, align_bytes=64)
-            copy_permuted(bf, raw[ORDER[k]][1], W3_SCALAR[k])
-            return quantize(bf[:], H, "w3", work, 3)
+            bf = slabs3.tile([P, PACK * H * 2], BF16, name="w3_bf%d" % k, offset=(k % R3) * 8192, align_bytes=64)
+            copy_permuted(bf, raw[ORDER[k]][1], W3_SCALAR[k], W3_GPSIMD[k], 1)
+            return quantize(bf[:, : PACK * H], H, "w3", work, WB)
 
         def weights2(e, at):
             if at is None:
                 bf = work.tile([P, N, PACK], BF16, name="w2_bf", tag="w2_bf", bufs=2, align_bytes=64)
             else:
-                bf = slabs1.tile([P, N, PACK], BF16, name="w2_bf%d" % e, offset=(at % 3) * 5120 + 4096, align_bytes=64)
+                bf = slabs1.tile([P, N, PACK], BF16, name="w2_bf%d" % e, offset=(at % R1) * 5120 + 4096, align_bytes=64)
             dst = bf[:].rearrange("p (c i) j -> p c j i", i=4)
             src = raw[e][2][:].rearrange("p j (c i) -> p c j i", i=4)
             if W2_ENGINE[e] == "V":
@@ -164,7 +199,7 @@ def tile_moe_shr_glu_sigmoid_kernel(tc, xT, w1, w3, w2, gate, offs, pos1, pos2, 
             return (x_codes[e // 2], (e % 2) * C)
 
         def gate_half(e, x, col, st):
-            a = product(w1q[e], x, col, "a_ps", 2)
+            a = product(w1q[e], x, col, "a_ps", ABUFS)
             nc.scalar.activation(out=st[:], in_=a, func=SIGMOID)
 
         def sigmoids(e, k):
@@ -173,7 +208,7 @@ def tile_moe_shr_glu_sigmoid_kernel(tc, xT, w1, w3, w2, gate, offs, pos1, pos2, 
                     st = work.tile([P, GROUP, PACK], F32, name="s_sh", tag="s_sh", bufs=8)
                 else:
                     st = slabs1.tile(
-                        [P, GROUP, PACK], F32, name="s%d_%d" % (e, g), offset=(k % 3) * 5120 + 2048 * g, align_bytes=64
+                        [P, GROUP, PACK], F32, name="s%d_%d" % (e, g), offset=(k % R1) * 5120 + 2048 * g, align_bytes=64
                     )
                 s[e, g] = st
                 x, base = x_of(e)
@@ -183,9 +218,11 @@ def tile_moe_shr_glu_sigmoid_kernel(tc, xT, w1, w3, w2, gate, offs, pos1, pos2, 
             if k is None:
                 hb = work.tile([P, C, PACK], BF16, name="hb", tag="hb", bufs=3, align_bytes=64)
             else:
-                hb = slabs3.tile([P, C, PACK], BF16, name="hb%d" % e, offset=(k % 3) * 4096, align_bytes=64)
+                hb = slabs3.tile([P, C, PACK], BF16, name="hb%d" % e, offset=(k % R3) * 8192, align_bytes=64)
+            x, base = x_of(e)
+            b = [product(w3q[e], x, base + g * GROUP, "b_ps", BBUFS) for g in range(2)]
             for g in range(2):
-                nc.vector.tensor_tensor(hb[:, g * GROUP : (g + 1) * GROUP, :], b[e][g], s[e, g][:], MULT)
+                nc.vector.tensor_tensor(hb[:, g * GROUP : (g + 1) * GROUP, :], b[g], s[e, g][:], MULT)
             hq[e] = quantize(hb[:].rearrange("p n j -> p (n j)"), 256, "h", work, 4)
 
         def second(w, h, ps, col):
@@ -217,56 +254,68 @@ def tile_moe_shr_glu_sigmoid_kernel(tc, xT, w1, w3, w2, gate, offs, pos1, pos2, 
                     hb = work.tile([P, C, PACK], BF16, name="hb", tag="hb", bufs=3, align_bytes=64)
                     for g in range(2):
                         n = i * 4 + h * 2 + g
-                        bt = product(w3q[E], shared["x"], n * GROUP, "b_ps", 4)
+                        bt = product(w3q[E], shared["x"], n * GROUP, "b_ps", BBUFS)
                         nc.vector.tensor_tensor(hb[:, g * GROUP : (g + 1) * GROUP, :], bt, s[E, n][:], MULT)
                     second(w2q[E], quantize(hb[:].rearrange("p n j -> p (n j)"), 256, "h", work, 4), y_ps, h * 256)
-                nc.scalar.copy(ys[:, i * 512 : (i + 1) * 512], y_ps[:])
+                (nc.scalar.copy if YS_ENGINE == "S" else nc.vector.tensor_copy)(ys[:, i * 512 : (i + 1) * 512], y_ps[:])
+
+        def at(k):
+            return ORDER[k] if 0 <= k <= E else None
+
+        def stage_sigmoids(i, k):
+            if at(i) == E:
+                shared_sigmoids()
+            elif at(i) is not None:
+                sigmoids(at(i), k)
+
+        def stage_hidden(i, k):
+            if at(i) == E:
+                shared_hidden()
+            elif at(i) is not None:
+                hidden(at(i), k)
+
+        def stage_results(i, k):
+            if at(i) is not None and at(i) < E:
+                w2q[at(i)] = weights2(at(i), k)
+                results(at(i))
 
         for k in range(E + 1):
             e = ORDER[k]
-            prev = ORDER[k - 1] if k >= 1 else None
             if e < E and e // 2 not in x_codes:
+                assert GATHER_AT[e // 2] < 0
                 gather(e // 2)
             w1q[e] = weights1(k)
-            if prev == E:
-                w2q[E] = weights2(E, k)
-                shared_sigmoids()
-            elif k >= 1:
-                sigmoids(prev, k)
-            if k >= 2 and ORDER[k - 2] < E:
-                w2q[ORDER[k - 2]] = weights2(ORDER[k - 2], k)
-                results(ORDER[k - 2])
+            if e == E:
+                w2q[E] = weights2(E, None)
+            stage_sigmoids(k - SLAG, k)
             w3q[e] = weights3(k)
-            if e < E:
-                x, base = x_of(e)
-                b[e] = [product(w3q[e], x, base + g * GROUP, "b_ps", 4) for g in range(2)]
-            if prev == E:
-                shared_hidden()
-            elif k >= 1:
-                hidden(prev, k)
-            if k + 3 <= E:
-                load(k + 3)
-            if k == 1:
+            for q in range(4):
+                if GATHER_AT[q] == k:
+                    gather(q)
+            stage_hidden(k - HLAG, k)
+            stage_results(k - W2LAG, k)
+            if k + LOAD_AHEAD <= E:
+                load(k + LOAD_AHEAD)
+            if k == XS_AT:
                 shared["x"] = quantize(x_shared[:].rearrange("p t j -> p (t j)"), T, "xs", keep, 1)
-        last = ORDER[E]
-        w2q[last] = weights2(last, None)
-        sigmoids(last, None)
-        prev = ORDER[E - 1]
-        w2q[prev] = weights2(prev, None)
-        hidden(last, None)
-        results(prev)
-        results(last)
+        for k in range(E + 1, E + 4):
+            if k - SLAG <= E:
+                stage_sigmoids(k - SLAG, None)
+            if k - HLAG <= E:
+                stage_hidden(k - HLAG, None)
+            if k - W2LAG <= E:
+                stage_results(k - W2LAG, None)
 
         r1 = keep.tile([P, T], F32, name="r1")
         r2 = keep.tile([P, T], F32, name="r2")
         r1s = keep.tile([P, T], F32, name="r1s")
-        W = T // 2
-        for i in range(2):
+        W = T // CHUNKS
+        for i in range(CHUNKS):
             cols = slice(i * W, (i + 1) * W)
             lst = slice(i * W // 16, (i + 1) * W // 16)
             nc.vector.tensor_tensor(r1[:, cols], y[:].indirect(pos1_sb[:, lst]), gate_sb[0][:, cols], MULT)
-            nc.gpsimd.tensor_tensor(r1s[:, cols], r1[:, cols], ys[:, cols], ADD)
-        for i in range(2):
+            (nc.vector if FIN[0] == "V" else nc.gpsimd).tensor_tensor(r1s[:, cols], r1[:, cols], ys[:, cols], ADD)
+        for i in range(CHUNKS):
             cols = slice(i * W, (i + 1) * W)
             lst = slice(i * W // 16, (i + 1) * W // 16)
             nc.vector.tensor_tensor(r2[:, cols], y[:].indirect(pos2_sb[:, lst]), gate_sb[1][:, cols], MULT)

@@ -19,30 +19,38 @@ P = 128
 PACK = 4
 GROUP = 128
 PAIR = 2 * C
-ORDER = [0,1,2,3,8,4,5,6,7]
-W3_SCALAR = [112,80,96,32,112,32,48,48,32]
-W2_ENGINE = ["G","V","G","G","S","S","V","S","G"]
-CAST = ["V","G","G","S"]
-W1_SCALAR = [112,112,112,128,128,128,128,128,112]
-W3_GPSIMD = [16,16,32,48,32,32,32,32,32]
+ORDER = [0, 1, 2, 3, 8, 4, 5, 6, 7]
+W3_SCALAR = [96, 80, 16, 80, 80, 80, 32, 96, 32]
+W2_ENGINE = ["S", "S", "S", "G", "S", "G", "G", "G", "S"]
+CAST = ["S", "V", "S", "S"]
+W1_SCALAR = [80, 112, 128, 128, 96, 96, 96, 96, 128]
+W3_GPSIMD = [48, 48, 48, 48, 48, 16, 48, 48, 16]
+W1_GPSIMD = [16, 32, 32, 16, 48, 48, 16, 32, 32]
+GATHER_MODE = ["step", "step", "step", "step"]
+XS_ENGINE = ["V", "G", "G", "V"]
+XS_TEXT = 2
 GP = 2
-SP = [2,2,2,2,2,2,1,1,1]
+SP = [2, 1, 1, 2, 2, 1, 1, 1, 2]
 CHUNKS = 2
 YS_ENGINE = "V"
-GATHER_AT = [-1,-1,3,2]
-XS_AT = 2
-FIN = ["V","V"]
+GATHER_AT = [-1, -1, 3, 2]
+XS_AT = 3
+FIN = ["G", "V"]
 SLAG = 1
 HLAG = 1
 W2LAG = 2
-R1 = 2
-R3 = 3
-WB = 4
-XB = 4
+SOVER = "raw"
+HOVER = "w3"
+RR = 3
+HSPLIT = 1
+R1 = 3
+R3 = 2
+WB = 3
+XB = 2
 ABUFS = 2
 BBUFS = 4
 LOAD_AHEAD = 3
-GATE_AT = 4
+GATE_AT = 7
 
 
 def tile_moe_shr_glu_sigmoid_kernel(tc, xT, w1, w3, w2, gate, offs, pos1, pos2, out):
@@ -50,6 +58,7 @@ def tile_moe_shr_glu_sigmoid_kernel(tc, xT, w1, w3, w2, gate, offs, pos1, pos2, 
     with ExitStack() as ctx:
         keep = ctx.enter_context(tc.tile_pool(name="keep", bufs=1))
         rawp = ctx.enter_context(tc.tile_pool(name="rawp", bufs=6))
+        rawp1 = ctx.enter_context(tc.tile_pool(name="rawp1", bufs=1))
         work = ctx.enter_context(tc.tile_pool(name="work", bufs=3))
         slabs1 = ctx.enter_context(tc.tile_pool(name="slabs1", bufs=1))
         slabs3 = ctx.enter_context(tc.tile_pool(name="slabs3", bufs=1))
@@ -61,13 +70,14 @@ def tile_moe_shr_glu_sigmoid_kernel(tc, xT, w1, w3, w2, gate, offs, pos1, pos2, 
         nc.scalar.activation(out=warm_out[:], in_=warm[:], func=SIGMOID)
 
         offs_sb = keep.tile([P, E * C // 16], U16, name="offs_sb")
-        nc.sync.dma_start(offs_sb[:], offs)
         x_raw = keep.tile([P, PACK, T], F32, name="x_raw")
         x_view = xT.rearrange("(p j) t -> p j t", j=PACK)
         for u in range(2):
             for half in range(2):
                 cols = slice(half * 512, half * 512 + 512)
                 nc.sync.dma_start(out=x_raw[:, 2 * u : 2 * u + 2, cols], in_=x_view[:, 2 * u : 2 * u + 2, cols])
+            if u == 0:
+                nc.sync.dma_start(offs_sb[:], offs)
         pos1_sb = keep.tile([P, T // 16], U16, name="pos1_sb")
         pos2_sb = keep.tile([P, T // 16], U16, name="pos2_sb")
         gate_sb = [keep.tile([P, T], F32, name="gate0"), keep.tile([P, T], F32, name="gate1")]
@@ -81,9 +91,9 @@ def tile_moe_shr_glu_sigmoid_kernel(tc, xT, w1, w3, w2, gate, offs, pos1, pos2, 
                 nc.sync.dma_start(pos2_sb[:], pos2)
                 for r in range(2):
                     nc.sync.dma_start(out=gate_sb[r][:], in_=gate[r])
-            r1 = rawp.tile([P, PACK, H], F32, name="w13_raw", tag="w13_raw")
+            r1 = rawp1.tile([P, PACK, H], F32, name="w1_raw%d" % k, offset=(k % RR) * 8192, align_bytes=64)
             nc.sync.dma_start(out=r1[:], in_=w1[e].rearrange("(p j) c -> p j c", j=PACK))
-            r3 = rawp.tile([P, PACK, H], F32, name="w13_raw", tag="w13_raw")
+            r3 = rawp.tile([P, PACK, H], F32, name="w3_raw", tag="w3_raw", bufs=3)
             nc.sync.dma_start(out=r3[:], in_=w3[e].rearrange("(p j) c -> p j c", j=PACK))
             r2 = rawp.tile([P, PACK, N], F32, name="w2_raw", tag="w2_raw", bufs=4)
             nc.sync.dma_start(out=r2[:], in_=w2[e].rearrange("(p j) c -> p j c", j=PACK))
@@ -108,10 +118,20 @@ def tile_moe_shr_glu_sigmoid_kernel(tc, xT, w1, w3, w2, gate, offs, pos1, pos2, 
             load(k)
 
         x_shared = keep.tile([P, T, PACK], BF16, name="x_shared", align_bytes=64)
-        for part in range(4):
-            dst = x_shared[:].rearrange("p (c i) j -> p c j i", i=4)[:, part * 64 : part * 64 + 64]
-            src = x_raw[:].rearrange("p j (c i) -> p c j i", i=4)[:, part * 64 : part * 64 + 64]
-            nc.gpsimd.tensor_scalar(dst, src, 1.0, 0.0, MULT, ADD)
+
+        def interleave_shared(part):
+            cols = slice(part * 256, part * 256 + 256)
+            dst = x_shared[:, cols, :]
+            src = x_raw[:, :, cols].rearrange("p j t -> p t j")
+            if XS_ENGINE[part] == "G":
+                nc.gpsimd.tensor_scalar(dst, src, 1.0, 0.0, MULT, ADD)
+            else:
+                dst = dst.rearrange("p (c i) j -> p c j i", i=4)
+                src = x_raw[:, :, cols].rearrange("p j (c i) -> p c j i", i=4)
+                if XS_ENGINE[part] == "V":
+                    nc.vector.tensor_copy(dst, src)
+                else:
+                    nc.scalar.copy(dst, src)
 
         x_codes = {}
 
@@ -129,10 +149,15 @@ def tile_moe_shr_glu_sigmoid_kernel(tc, xT, w1, w3, w2, gate, offs, pos1, pos2, 
                 g = slabs3.tile([P, PAIR, PACK], BF16, name="gathered%d" % q, offset=(at % R3) * 8192 + 4096, align_bytes=64)
             words = g[:].rearrange("p s j -> p (s j)").bitcast(U32).rearrange("p (s u) -> p s u", u=2)
             for u in range(2):
-                nc.vector.tensor_copy(
-                    words[:, :, u],
-                    windows[u][:].bitcast(U32).indirect(offs_sb[:, q * PAIR // 16 : (q + 1) * PAIR // 16]),
-                )
+                picked = windows[u][:].bitcast(U32).indirect(offs_sb[:, q * PAIR // 16 : (q + 1) * PAIR // 16])
+                if GATHER_MODE[q] == "step":
+                    nc.vector.tensor_copy(words[:, :, u], picked)
+                else:
+                    plane = work.tile([P, PAIR * 2], BF16, name="plane", tag="plane", bufs=2, align_bytes=64)
+                    nc.vector.tensor_copy(plane[:].bitcast(U32), picked)
+                    nc.gpsimd.tensor_scalar(
+                        g[:, :, 2 * u : 2 * u + 2], plane[:].rearrange("p (s e) -> p s e", e=2), 1.0, 0.0, MULT, ADD
+                    )
             x_codes[q] = quantize(g[:].rearrange("p s j -> p (s j)"), PAIR, "x", work, XB)
 
         def copy_permuted(dst_tile, src_tile, m_scalar, m_gpsimd, pieces):
@@ -149,11 +174,18 @@ def tile_moe_shr_glu_sigmoid_kernel(tc, xT, w1, w3, w2, gate, offs, pos1, pos2, 
                 step = (128 - m_vector) // GP
                 for i in range(GP):
                     a = m_vector + i * step
-                    nc.gpsimd.tensor_scalar(dst[:, a : a + step], src[:, a : a + step], 1.0, 0.0, MULT, ADD)
+                    nc.gpsimd.tensor_scalar(
+                        dst_tile[:, : PACK * H].rearrange("p (t m j) -> p t m j", t=4, j=PACK)[:, :, a : a + step],
+                        src_tile[:].rearrange("p j (m t) -> p t m j", t=4)[:, :, a : a + step],
+                        1.0,
+                        0.0,
+                        MULT,
+                        ADD,
+                    )
 
         def weights1(k):
             bf = slabs1.tile([P, PACK * H + 512], BF16, name="w1_bf%d" % k, offset=(k % R1) * 5120, align_bytes=64)
-            copy_permuted(bf, raw[ORDER[k]][0], W1_SCALAR[k], 0, SP[k])
+            copy_permuted(bf, raw[ORDER[k]][0], W1_SCALAR[k], W1_GPSIMD[k], SP[k])
             return quantize(bf[:, : PACK * H], H, "w1", work, WB)
 
         def weights3(k):
@@ -173,7 +205,7 @@ def tile_moe_shr_glu_sigmoid_kernel(tc, xT, w1, w3, w2, gate, offs, pos1, pos2, 
             elif W2_ENGINE[e] == "S":
                 nc.scalar.copy(dst, src)
             else:
-                nc.gpsimd.tensor_scalar(dst, src, 1.0, 0.0, MULT, ADD)
+                nc.gpsimd.tensor_scalar(bf[:], raw[e][2][:].rearrange("p j c -> p c j"), 1.0, 0.0, MULT, ADD)
             return quantize(bf[:].rearrange("p c j -> p (c j)"), N, "w2", work, 4)
 
         def product(w, x, col, tag, bufs):
@@ -206,6 +238,10 @@ def tile_moe_shr_glu_sigmoid_kernel(tc, xT, w1, w3, w2, gate, offs, pos1, pos2, 
             for g in range(2):
                 if k is None:
                     st = work.tile([P, GROUP, PACK], F32, name="s_sh", tag="s_sh", bufs=8)
+                elif SOVER == "raw":
+                    st = rawp1.tile(
+                        [P, GROUP, PACK], F32, name="s%d_%d" % (e, g), offset=(k % RR) * 8192 + 2048 * g, align_bytes=64
+                    )
                 else:
                     st = slabs1.tile(
                         [P, GROUP, PACK], F32, name="s%d_%d" % (e, g), offset=(k % R1) * 5120 + 2048 * g, align_bytes=64
@@ -214,27 +250,44 @@ def tile_moe_shr_glu_sigmoid_kernel(tc, xT, w1, w3, w2, gate, offs, pos1, pos2, 
                 x, base = x_of(e)
                 gate_half(e, x, base + g * GROUP, st)
 
+        def quantize_hidden(hb):
+            flat = hb[:].rearrange("p n j -> p (n j)")
+            codes = work.tile([P, C], U32, name="h_codes", tag="h_codes", bufs=4, align_bytes=64)
+            scales = work.tile([P, C], U8, name="h_scales", tag="h_scales", bufs=4, align_bytes=64)
+            n = C // HSPLIT
+            for i in range(HSPLIT):
+                nc.vector.quantize_mx(
+                    out=codes[:, i * n : (i + 1) * n].bitcast(FP8X4),
+                    scales=scales[:, i * n : (i + 1) * n],
+                    in_=flat[:, i * n * PACK : (i + 1) * n * PACK],
+                )
+            return codes, scales
+
         def hidden(e, k):
             if k is None:
                 hb = work.tile([P, C, PACK], BF16, name="hb", tag="hb", bufs=3, align_bytes=64)
+            elif HOVER == "w1":
+                hb = slabs1.tile([P, C, PACK], BF16, name="hb%d" % e, offset=(k % R1) * 5120, align_bytes=64)
             else:
                 hb = slabs3.tile([P, C, PACK], BF16, name="hb%d" % e, offset=(k % R3) * 8192, align_bytes=64)
             x, base = x_of(e)
             b = [product(w3q[e], x, base + g * GROUP, "b_ps", BBUFS) for g in range(2)]
             for g in range(2):
                 nc.vector.tensor_tensor(hb[:, g * GROUP : (g + 1) * GROUP, :], b[g], s[e, g][:], MULT)
-            hq[e] = quantize(hb[:].rearrange("p n j -> p (n j)"), 256, "h", work, 4)
+            hq[e] = quantize_hidden(hb)
 
         def second(w, h, ps, col):
-            nc.tensor.matmul_mx(
-                out=ps[:, col : col + 256],
-                lhsT=w[0][:].bitcast(FP8X4),
-                lhsT_scale=w[1][:],
-                rhs=h[0][:].bitcast(FP8X4),
-                rhs_scale=h[1][:],
-                start=True,
-                stop=True,
-            )
+            n = C // HSPLIT
+            for i in range(HSPLIT):
+                nc.tensor.matmul_mx(
+                    out=ps[:, col + i * n : col + (i + 1) * n],
+                    lhsT=w[0][:].bitcast(FP8X4),
+                    lhsT_scale=w[1][:],
+                    rhs=h[0][:, i * n : (i + 1) * n].bitcast(FP8X4),
+                    rhs_scale=h[1][:, i * n : (i + 1) * n],
+                    start=True,
+                    stop=True,
+                )
 
         def results(e):
             y_ps = psum.tile([P, 512], F32, name="y_ps", tag="y_ps", bufs=2)
@@ -256,7 +309,7 @@ def tile_moe_shr_glu_sigmoid_kernel(tc, xT, w1, w3, w2, gate, offs, pos1, pos2, 
                         n = i * 4 + h * 2 + g
                         bt = product(w3q[E], shared["x"], n * GROUP, "b_ps", BBUFS)
                         nc.vector.tensor_tensor(hb[:, g * GROUP : (g + 1) * GROUP, :], bt, s[E, n][:], MULT)
-                    second(w2q[E], quantize(hb[:].rearrange("p n j -> p (n j)"), 256, "h", work, 4), y_ps, h * 256)
+                    second(w2q[E], quantize_hidden(hb), y_ps, h * 256)
                 (nc.scalar.copy if YS_ENGINE == "S" else nc.vector.tensor_copy)(ys[:, i * 512 : (i + 1) * 512], y_ps[:])
 
         def at(k):
@@ -296,6 +349,9 @@ def tile_moe_shr_glu_sigmoid_kernel(tc, xT, w1, w3, w2, gate, offs, pos1, pos2, 
             stage_results(k - W2LAG, k)
             if k + LOAD_AHEAD <= E:
                 load(k + LOAD_AHEAD)
+            if k == XS_TEXT:
+                for part in range(4):
+                    interleave_shared(part)
             if k == XS_AT:
                 shared["x"] = quantize(x_shared[:].rearrange("p t j -> p (t j)"), T, "xs", keep, 1)
         for k in range(E + 1, E + 4):

@@ -20,22 +20,22 @@ PACK = 4
 GROUP = 128
 PAIR = 2 * C
 ORDER = [0, 1, 2, 3, 8, 4, 5, 6, 7]
-W3_SCALAR = [96, 80, 16, 80, 80, 80, 32, 96, 32]
-W2_ENGINE = ["S", "S", "S", "G", "S", "G", "G", "G", "S"]
-CAST = ["S", "V", "S", "S"]
-W1_SCALAR = [80, 112, 128, 128, 96, 96, 96, 96, 128]
-W3_GPSIMD = [48, 48, 48, 48, 48, 16, 48, 48, 16]
-W1_GPSIMD = [16, 32, 32, 16, 48, 48, 16, 32, 32]
+W3_SCALAR = [128, 48, 64, 80, 96, 80, 80, 96, 32]
+W2_ENGINE = ["S", "S", "S", "G", "S", "G", "G", "S", "G"]
+CAST = ["V", "S", "V", "S"]
+W1_SCALAR = [64, 112, 128, 128, 96, 96, 32, 96, 128]
+W3_GPSIMD = [16, 48, 48, 32, 32, 32, 0, 0, 48]
+W1_GPSIMD = [48, 16, 16, 48, 48, 48, 48, 48, 48]
 GATHER_MODE = ["step", "step", "step", "step"]
-XS_ENGINE = ["V", "G", "G", "V"]
-XS_TEXT = 2
+XS_ENGINE = ["G", "S", "V", "S"]
+XS_TEXT = 1
 GP = 2
-SP = [2, 1, 1, 2, 2, 1, 1, 1, 2]
+SP = [1, 1, 1, 2, 2, 2, 2, 1, 2]
 CHUNKS = 2
 YS_ENGINE = "V"
-GATHER_AT = [-1, -1, 3, 2]
-XS_AT = 3
-FIN = ["G", "V"]
+GATHER_AT = [-1, 0, 3, 2]
+XS_AT = 1
+FIN = ["V", "V"]
 SLAG = 1
 HLAG = 1
 W2LAG = 2
@@ -43,14 +43,14 @@ SOVER = "raw"
 HOVER = "w3"
 RR = 3
 HSPLIT = 1
-R1 = 3
+R1 = 2
 R3 = 2
 WB = 3
 XB = 2
 ABUFS = 2
 BBUFS = 4
 LOAD_AHEAD = 3
-GATE_AT = 7
+GATE_AT = 3
 
 
 def tile_moe_shr_glu_sigmoid_kernel(tc, xT, w1, w3, w2, gate, offs, pos1, pos2, out):
@@ -121,17 +121,14 @@ def tile_moe_shr_glu_sigmoid_kernel(tc, xT, w1, w3, w2, gate, offs, pos1, pos2, 
 
         def interleave_shared(part):
             cols = slice(part * 256, part * 256 + 256)
-            dst = x_shared[:, cols, :]
-            src = x_raw[:, :, cols].rearrange("p j t -> p t j")
+            dst = x_shared[:, cols, :].rearrange("p (c i) j -> p c j i", i=4)
+            src = x_raw[:, :, cols].rearrange("p j (c i) -> p c j i", i=4)
             if XS_ENGINE[part] == "G":
                 nc.gpsimd.tensor_scalar(dst, src, 1.0, 0.0, MULT, ADD)
+            elif XS_ENGINE[part] == "V":
+                nc.vector.tensor_copy(dst, src)
             else:
-                dst = dst.rearrange("p (c i) j -> p c j i", i=4)
-                src = x_raw[:, :, cols].rearrange("p j (c i) -> p c j i", i=4)
-                if XS_ENGINE[part] == "V":
-                    nc.vector.tensor_copy(dst, src)
-                else:
-                    nc.scalar.copy(dst, src)
+                nc.scalar.copy(dst, src)
 
         x_codes = {}
 
@@ -174,14 +171,7 @@ def tile_moe_shr_glu_sigmoid_kernel(tc, xT, w1, w3, w2, gate, offs, pos1, pos2, 
                 step = (128 - m_vector) // GP
                 for i in range(GP):
                     a = m_vector + i * step
-                    nc.gpsimd.tensor_scalar(
-                        dst_tile[:, : PACK * H].rearrange("p (t m j) -> p t m j", t=4, j=PACK)[:, :, a : a + step],
-                        src_tile[:].rearrange("p j (m t) -> p t m j", t=4)[:, :, a : a + step],
-                        1.0,
-                        0.0,
-                        MULT,
-                        ADD,
-                    )
+                    nc.gpsimd.tensor_scalar(dst[:, a : a + step], src[:, a : a + step], 1.0, 0.0, MULT, ADD)
 
         def weights1(k):
             bf = slabs1.tile([P, PACK * H + 512], BF16, name="w1_bf%d" % k, offset=(k % R1) * 5120, align_bytes=64)
@@ -205,7 +195,7 @@ def tile_moe_shr_glu_sigmoid_kernel(tc, xT, w1, w3, w2, gate, offs, pos1, pos2, 
             elif W2_ENGINE[e] == "S":
                 nc.scalar.copy(dst, src)
             else:
-                nc.gpsimd.tensor_scalar(bf[:], raw[e][2][:].rearrange("p j c -> p c j"), 1.0, 0.0, MULT, ADD)
+                nc.gpsimd.tensor_scalar(dst, src, 1.0, 0.0, MULT, ADD)
             return quantize(bf[:].rearrange("p c j -> p (c j)"), N, "w2", work, 4)
 
         def product(w, x, col, tag, bufs):

from contextlib import ExitStack

import concourse.mybir as mybir

K, T, E, C, H, N = 512, 1024, 8, 256, 512, 128
FLOPS = 3623878656

F32 = mybir.dt.float32
BF16 = mybir.dt.bfloat16
U32 = mybir.dt.uint32
U16 = mybir.dt.uint16
U8 = mybir.dt.uint8
FP8X4 = mybir.dt.float8_e4m3fn_x4
SIGMOID = mybir.ActivationFunctionType.Sigmoid
MULT = mybir.AluOpType.mult
ADD = mybir.AluOpType.add

P = 128
PACK = 4
GROUP = 128
PAIR = 2 * C
ORDER = [0, 1, 2, 3, 8, 4, 5, 6, 7]
W3_SCALAR = [128, 48, 64, 80, 96, 80, 80, 96, 32]
W2_ENGINE = ["S", "S", "S", "G", "S", "G", "G", "S", "G"]
CAST = ["V", "S", "V", "S"]
W1_SCALAR = [64, 112, 128, 128, 96, 96, 32, 96, 128]
W3_GPSIMD = [16, 48, 48, 32, 32, 32, 0, 0, 48]
W1_GPSIMD = [48, 16, 16, 48, 48, 48, 48, 48, 48]
GATHER_MODE = ["step", "step", "step", "step"]
XS_ENGINE = ["G", "S", "V", "S"]
XS_TEXT = 1
GP = 2
SP = [1, 1, 1, 2, 2, 2, 2, 1, 2]
CHUNKS = 2
YS_ENGINE = "V"
GATHER_AT = [-1, 0, 3, 2]
XS_AT = 1
FIN = ["V", "V"]
SLAG = 1
HLAG = 1
W2LAG = 2
SOVER = "raw"
HOVER = "w3"
RR = 3
HSPLIT = 1
R1 = 2
R3 = 2
WB = 3
XB = 2
ABUFS = 2
BBUFS = 4
LOAD_AHEAD = 3
GATE_AT = 3


def tile_moe_shr_glu_sigmoid_kernel(tc, xT, w1, w3, w2, gate, offs, pos1, pos2, out):
    nc = tc.nc
    with ExitStack() as ctx:
        keep = ctx.enter_context(tc.tile_pool(name="keep", bufs=1))
        rawp = ctx.enter_context(tc.tile_pool(name="rawp", bufs=6))
        rawp1 = ctx.enter_context(tc.tile_pool(name="rawp1", bufs=1))
        work = ctx.enter_context(tc.tile_pool(name="work", bufs=3))
        slabs1 = ctx.enter_context(tc.tile_pool(name="slabs1", bufs=1))
        slabs3 = ctx.enter_context(tc.tile_pool(name="slabs3", bufs=1))
        psum = ctx.enter_context(tc.psum_pool(name="psum", bufs=2))

        warm = keep.tile([P, 1], F32, name="warm")
        warm_out = keep.tile([P, 1], F32, name="warm_out")
        nc.gpsimd.memset(warm[:], 0.0)
        nc.scalar.activation(out=warm_out[:], in_=warm[:], func=SIGMOID)

        offs_sb = keep.tile([P, E * C // 16], U16, name="offs_sb")
        x_raw = keep.tile([P, PACK, T], F32, name="x_raw")
        x_view = xT.rearrange("(p j) t -> p j t", j=PACK)
        for u in range(2):
            for half in range(2):
                cols = slice(half * 512, half * 512 + 512)
                nc.sync.dma_start(out=x_raw[:, 2 * u : 2 * u + 2, cols], in_=x_view[:, 2 * u : 2 * u + 2, cols])
            if u == 0:
                nc.sync.dma_start(offs_sb[:], offs)
        pos1_sb = keep.tile([P, T // 16], U16, name="pos1_sb")
        pos2_sb = keep.tile([P, T // 16], U16, name="pos2_sb")
        gate_sb = [keep.tile([P, T], F32, name="gate0"), keep.tile([P, T], F32, name="gate1")]

        raw = {}

        def load(k):
            e = ORDER[k]
            if k == GATE_AT:
                nc.sync.dma_start(pos1_sb[:], pos1)
                nc.sync.dma_start(pos2_sb[:], pos2)
                for r in range(2):
                    nc.sync.dma_start(out=gate_sb[r][:], in_=gate[r])
            r1 = rawp1.tile([P, PACK, H], F32, name="w1_raw%d" % k, offset=(k % RR) * 8192, align_bytes=64)
            nc.sync.dma_start(out=r1[:], in_=w1[e].rearrange("(p j) c -> p j c", j=PACK))
            r3 = rawp.tile([P, PACK, H], F32, name="w3_raw", tag="w3_raw", bufs=3)
            nc.sync.dma_start(out=r3[:], in_=w3[e].rearrange("(p j) c -> p j c", j=PACK))
            r2 = rawp.tile([P, PACK, N], F32, name="w2_raw", tag="w2_raw", bufs=4)
            nc.sync.dma_start(out=r2[:], in_=w2[e].rearrange("(p j) c -> p j c", j=PACK))
            raw[e] = (r1, r3, r2)

        windows = []
        for u in range(2):
            win = keep.tile([P, 2 * T], BF16, name="win%d" % u)
            dst = win[:].rearrange("p (t e) -> p t e", e=2)
            src = x_raw[:, 2 * u : 2 * u + 2, :].rearrange("p e t -> p t e")
            for half in range(2):
                cols = slice(half * 512, half * 512 + 512)
                if CAST[2 * u + half] == "V":
                    nc.vector.tensor_copy(dst[:, cols, :], src[:, cols, :])
                elif CAST[2 * u + half] == "G":
                    nc.gpsimd.tensor_scalar(dst[:, cols, :], src[:, cols, :], 1.0, 0.0, MULT, ADD)
                else:
                    nc.scalar.copy(dst[:, cols, :], src[:, cols, :])
            windows.append(win)

        for k in range(LOAD_AHEAD):
            load(k)

        x_shared = keep.tile([P, T, PACK], BF16, name="x_shared", align_bytes=64)

        def interleave_shared(part):
            cols = slice(part * 256, part * 256 + 256)
            dst = x_shared[:, cols, :].rearrange("p (c i) j -> p c j i", i=4)
            src = x_raw[:, :, cols].rearrange("p j (c i) -> p c j i", i=4)
            if XS_ENGINE[part] == "G":
                nc.gpsimd.tensor_scalar(dst, src, 1.0, 0.0, MULT, ADD)
            elif XS_ENGINE[part] == "V":
                nc.vector.tensor_copy(dst, src)
            else:
                nc.scalar.copy(dst, src)

        x_codes = {}

        def quantize(src, width, name, pool, bufs):
            codes = pool.tile([P, width], U32, name=name + "_codes", tag=name + "_codes", bufs=bufs, align_bytes=64)
            scales = pool.tile([P, width], U8, name=name + "_scales", tag=name + "_scales", bufs=bufs, align_bytes=64)
            nc.vector.quantize_mx(out=codes[:].bitcast(FP8X4), scales=scales[:], in_=src)
            return codes, scales

        def gather(q):
            at = GATHER_AT[q]
            if at < 0:
                g = work.tile([P, PAIR, PACK], BF16, name="gathered", tag="gathered", bufs=1, align_bytes=64)
            else:
                g = slabs3.tile([P, PAIR, PACK], BF16, name="gathered%d" % q, offset=(at % R3) * 8192 + 4096, align_bytes=64)
            words = g[:].rearrange("p s j -> p (s j)").bitcast(U32).rearrange("p (s u) -> p s u", u=2)
            for u in range(2):
                picked = windows[u][:].bitcast(U32).indirect(offs_sb[:, q * PAIR // 16 : (q + 1) * PAIR // 16])
                if GATHER_MODE[q] == "step":
                    nc.vector.tensor_copy(words[:, :, u], picked)
                else:
                    plane = work.tile([P, PAIR * 2], BF16, name="plane", tag="plane", bufs=2, align_bytes=64)
                    nc.vector.tensor_copy(plane[:].bitcast(U32), picked)
                    nc.gpsimd.tensor_scalar(
                        g[:, :, 2 * u : 2 * u + 2], plane[:].rearrange("p (s e) -> p s e", e=2), 1.0, 0.0, MULT, ADD
                    )
            x_codes[q] = quantize(g[:].rearrange("p s j -> p (s j)"), PAIR, "x", work, XB)

        def copy_permuted(dst_tile, src_tile, m_scalar, m_gpsimd, pieces):
            dst = dst_tile[:, : PACK * H].rearrange("p (t m j) -> p m j t", t=4, j=PACK)
            src = src_tile[:].rearrange("p j (m t) -> p m j t", t=4)
            m_vector = max(m_scalar, 128 - m_gpsimd)
            if m_scalar > 0:
                step = m_scalar // pieces
                for i in range(pieces):
                    nc.scalar.copy(dst[:, i * step : (i + 1) * step], src[:, i * step : (i + 1) * step])
            if m_scalar < m_vector:
                nc.vector.tensor_copy(dst[:, m_scalar:m_vector], src[:, m_scalar:m_vector])
            if m_vector < 128:
                step = (128 - m_vector) // GP
                for i in range(GP):
                    a = m_vector + i * step
                    nc.gpsimd.tensor_scalar(dst[:, a : a + step], src[:, a : a + step], 1.0, 0.0, MULT, ADD)

        def weights1(k):
            bf = slabs1.tile([P, PACK * H + 512], BF16, name="w1_bf%d" % k, offset=(k % R1) * 5120, align_bytes=64)
            copy_permuted(bf, raw[ORDER[k]][0], W1_SCALAR[k], W1_GPSIMD[k], SP[k])
            return quantize(bf[:, : PACK * H], H, "w1", work, WB)

        def weights3(k):
            bf = slabs3.tile([P, PACK * H * 2], BF16, name="w3_bf%d" % k, offset=(k % R3) * 8192, align_bytes=64)
            copy_permuted(bf, raw[ORDER[k]][1], W3_SCALAR[k], W3_GPSIMD[k], 1)
            return quantize(bf[:, : PACK * H], H, "w3", work, WB)

        def weights2(e, at):
            if at is None:
                bf = work.tile([P, N, PACK], BF16, name="w2_bf", tag="w2_bf", bufs=2, align_bytes=64)
            else:
                bf = slabs1.tile([P, N, PACK], BF16, name="w2_bf%d" % e, offset=(at % R1) * 5120 + 4096, align_bytes=64)
            dst = bf[:].rearrange("p (c i) j -> p c j i", i=4)
            src = raw[e][2][:].rearrange("p j (c i) -> p c j i", i=4)
            if W2_ENGINE[e] == "V":
                nc.vector.tensor_copy(dst, src)
            elif W2_ENGINE[e] == "S":
                nc.scalar.copy(dst, src)
            else:
                nc.gpsimd.tensor_scalar(dst, src, 1.0, 0.0, MULT, ADD)
            return quantize(bf[:].rearrange("p c j -> p (c j)"), N, "w2", work, 4)

        def product(w, x, col, tag, bufs):
            ps = psum.tile([P, PACK * GROUP], F32, name=tag, tag=tag, bufs=bufs)
            for t in range(4):
                nc.tensor.matmul_mx(
                    out=ps[:, t * GROUP : (t + 1) * GROUP],
                    lhsT=w[0][:, t * 128 : (t + 1) * 128].bitcast(FP8X4),
                    lhsT_scale=w[1][:, t * 128 : (t + 1) * 128],
                    rhs=x[0][:, col : col + GROUP].bitcast(FP8X4),
                    rhs_scale=x[1][:, col : col + GROUP],
                    start=True,
                    stop=True,
                )
            return ps[:].rearrange("p (j n) -> p n j", j=PACK)

        y = keep.tile([P, E * C], F32, name="y")
        ys = keep.tile([P, T], F32, name="ys")
        w1q, w3q, w2q, b, hq, s = {}, {}, {}, {}, {}, {}
        shared = {}

        def x_of(e):
            return (x_codes[e // 2], (e % 2) * C)

        def gate_half(e, x, col, st):
            a = product(w1q[e], x, col, "a_ps", ABUFS)
            nc.scalar.activation(out=st[:], in_=a, func=SIGMOID)

        def sigmoids(e, k):
            for g in range(2):
                if k is None:
                    st = work.tile([P, GROUP, PACK], F32, name="s_sh", tag="s_sh", bufs=8)
                elif SOVER == "raw":
                    st = rawp1.tile(
                        [P, GROUP, PACK], F32, name="s%d_%d" % (e, g), offset=(k % RR) * 8192 + 2048 * g, align_bytes=64
                    )
                else:
                    st = slabs1.tile(
                        [P, GROUP, PACK], F32, name="s%d_%d" % (e, g), offset=(k % R1) * 5120 + 2048 * g, align_bytes=64
                    )
                s[e, g] = st
                x, base = x_of(e)
                gate_half(e, x, base + g * GROUP, st)

        def quantize_hidden(hb):
            flat = hb[:].rearrange("p n j -> p (n j)")
            codes = work.tile([P, C], U32, name="h_codes", tag="h_codes", bufs=4, align_bytes=64)
            scales = work.tile([P, C], U8, name="h_scales", tag="h_scales", bufs=4, align_bytes=64)
            n = C // HSPLIT
            for i in range(HSPLIT):
                nc.vector.quantize_mx(
                    out=codes[:, i * n : (i + 1) * n].bitcast(FP8X4),
                    scales=scales[:, i * n : (i + 1) * n],
                    in_=flat[:, i * n * PACK : (i + 1) * n * PACK],
                )
            return codes, scales

        def hidden(e, k):
            if k is None:
                hb = work.tile([P, C, PACK], BF16, name="hb", tag="hb", bufs=3, align_bytes=64)
            elif HOVER == "w1":
                hb = slabs1.tile([P, C, PACK], BF16, name="hb%d" % e, offset=(k % R1) * 5120, align_bytes=64)
            else:
                hb = slabs3.tile([P, C, PACK], BF16, name="hb%d" % e, offset=(k % R3) * 8192, align_bytes=64)
            x, base = x_of(e)
            b = [product(w3q[e], x, base + g * GROUP, "b_ps", BBUFS) for g in range(2)]
            for g in range(2):
                nc.vector.tensor_tensor(hb[:, g * GROUP : (g + 1) * GROUP, :], b[g], s[e, g][:], MULT)
            hq[e] = quantize_hidden(hb)

        def second(w, h, ps, col):
            n = C // HSPLIT
            for i in range(HSPLIT):
                nc.tensor.matmul_mx(
                    out=ps[:, col + i * n : col + (i + 1) * n],
                    lhsT=w[0][:].bitcast(FP8X4),
                    lhsT_scale=w[1][:],
                    rhs=h[0][:, i * n : (i + 1) * n].bitcast(FP8X4),
                    rhs_scale=h[1][:, i * n : (i + 1) * n],
                    start=True,
                    stop=True,
                )

        def results(e):
            y_ps = psum.tile([P, 512], F32, name="y_ps", tag="y_ps", bufs=2)
            second(w2q[e], hq[e], y_ps, 0)
            nc.scalar.copy(y[:, e * C : (e + 1) * C], y_ps[:, :C])

        def shared_sigmoids():
            for g in range(T // GROUP):
                st = work.tile([P, GROUP, PACK], F32, name="s_sh", tag="s_sh", bufs=8)
                gate_half(E, shared["x"], g * GROUP, st)
                s[E, g] = st

        def shared_hidden():
            for i in range(T // 512):
                y_ps = psum.tile([P, 512], F32, name="y_ps", tag="y_ps", bufs=2)
                for h in range(2):
                    hb = work.tile([P, C, PACK], BF16, name="hb", tag="hb", bufs=3, align_bytes=64)
                    for g in range(2):
                        n = i * 4 + h * 2 + g
                        bt = product(w3q[E], shared["x"], n * GROUP, "b_ps", BBUFS)
                        nc.vector.tensor_tensor(hb[:, g * GROUP : (g + 1) * GROUP, :], bt, s[E, n][:], MULT)
                    second(w2q[E], quantize_hidden(hb), y_ps, h * 256)
                (nc.scalar.copy if YS_ENGINE == "S" else nc.vector.tensor_copy)(ys[:, i * 512 : (i + 1) * 512], y_ps[:])

        def at(k):
            return ORDER[k] if 0 <= k <= E else None

        def stage_sigmoids(i, k):
            if at(i) == E:
                shared_sigmoids()
            elif at(i) is not None:
                sigmoids(at(i), k)

        def stage_hidden(i, k):
            if at(i) == E:
                shared_hidden()
            elif at(i) is not None:
                hidden(at(i), k)

        def stage_results(i, k):
            if at(i) is not None and at(i) < E:
                w2q[at(i)] = weights2(at(i), k)
                results(at(i))

        for k in range(E + 1):
            e = ORDER[k]
            if e < E and e // 2 not in x_codes:
                assert GATHER_AT[e // 2] < 0
                gather(e // 2)
            w1q[e] = weights1(k)
            if e == E:
                w2q[E] = weights2(E, None)
            stage_sigmoids(k - SLAG, k)
            w3q[e] = weights3(k)
            for q in range(4):
                if GATHER_AT[q] == k:
                    gather(q)
            stage_hidden(k - HLAG, k)
            stage_results(k - W2LAG, k)
            if k + LOAD_AHEAD <= E:
                load(k + LOAD_AHEAD)
            if k == XS_TEXT:
                for part in range(4):
                    interleave_shared(part)
            if k == XS_AT:
                shared["x"] = quantize(x_shared[:].rearrange("p t j -> p (t j)"), T, "xs", keep, 1)
        for k in range(E + 1, E + 4):
            if k - SLAG <= E:
                stage_sigmoids(k - SLAG, None)
            if k - HLAG <= E:
                stage_hidden(k - HLAG, None)
            if k - W2LAG <= E:
                stage_results(k - W2LAG, None)

        r1 = keep.tile([P, T], F32, name="r1")
        r2 = keep.tile([P, T], F32, name="r2")
        r1s = keep.tile([P, T], F32, name="r1s")
        W = T // CHUNKS
        for i in range(CHUNKS):
            cols = slice(i * W, (i + 1) * W)
            lst = slice(i * W // 16, (i + 1) * W // 16)
            nc.vector.tensor_tensor(r1[:, cols], y[:].indirect(pos1_sb[:, lst]), gate_sb[0][:, cols], MULT)
            (nc.vector if FIN[0] == "V" else nc.gpsimd).tensor_tensor(r1s[:, cols], r1[:, cols], ys[:, cols], ADD)
        for i in range(CHUNKS):
            cols = slice(i * W, (i + 1) * W)
            lst = slice(i * W // 16, (i + 1) * W // 16)
            nc.vector.tensor_tensor(r2[:, cols], y[:].indirect(pos2_sb[:, lst]), gate_sb[1][:, cols], MULT)
            o = work.tile([P, W], F32, name="o", tag="o", bufs=2)
            nc.vector.tensor_tensor(o[:], r2[:, cols], r1s[:, cols], ADD)
            nc.sync.dma_start(out=out[:, cols], in_=o[:])
